import numpy as np
import ml_dtypes


def mxq(x, axis, fmt="e4m3"):
    dtype, down = {"e4m3": (ml_dtypes.float8_e4m3fn, 7), "e5m2": (ml_dtypes.float8_e5m2, 14)}[fmt]
    v = np.moveaxis(np.asarray(x, np.float32).astype(ml_dtypes.bfloat16).astype(np.float64), axis, -1)
    blocks = v.reshape(v.shape[:-1] + (-1, 32))
    amax = np.abs(blocks).max(-1, keepdims=True)
    byte = np.maximum(np.where(amax > 0, np.frexp(amax)[1] - 1 + 127, 0) - down, 1)
    scale = np.exp2(byte - 127.0)
    codes = (blocks / scale).astype(np.float32).astype(dtype).astype(np.float64)
    return np.moveaxis((codes * scale).reshape(v.shape), -1, axis)


WIDE = False


def mx_kscale(k):
    if not WIDE:
        return np.ones(k)
    levels = np.array([10, -10, 5, -5, 0])
    if k % 512:
        return np.exp2(np.random.permutation(np.resize(levels, k // 32))).repeat(32)
    a = np.empty((k // 512, 16))
    for p in range(k // 512):
        a[p, :8] = np.random.permutation(np.resize(levels, 8))
        for g in range(8):
            far = levels[np.abs(levels - a[p, g]) >= 10]
            a[p, g + 8] = far[np.random.randint(len(far))]
    return np.exp2(a.ravel()).repeat(32)


def f64(x):
    return np.asarray(x).astype(np.float64)


def striped(idx):
    return np.tile(idx.reshape(-1, 16).T, (8, 1)).astype(np.uint16)


def unstriped(offs):
    return offs[:16].T.reshape(-1).astype(np.int64)


def striped8(idx):
    return np.concatenate([x.reshape(-1, 16).T for x in idx]).astype(np.uint16)


def runs(offs, k):
    lists = np.stack([offs[16 * r : 16 * r + 16].T.reshape(-1) for r in range(8)]).astype(np.int64)
    return lists[np.arange(k) % 512 // 64]


def pack_weight(w):
    k, n = w.shape
    w = f64(np.asarray(w, np.float32).astype(ml_dtypes.bfloat16)).reshape(k // 32, 32, n)
    amax = np.abs(w).max(1)
    byte = np.clip(np.where(amax > 0, np.frexp(amax)[1] - 1 + 127 - 7, 1), 1, 254)
    scaled = (w * np.exp2(127.0 - byte)[:, None, :]).reshape(k, n).astype(np.float32)
    words = np.ascontiguousarray(scaled.reshape(k // 512, 128, 4, n).transpose(0, 1, 3, 2)).astype(ml_dtypes.float8_e4m3fn).view(np.uint8)
    return words, np.ascontiguousarray(byte.astype(np.uint8).reshape(k // 512, 16, n))


def unpack_weight(words, scales):
    g, p, n, _ = words.shape
    vals = np.ascontiguousarray(words).view(ml_dtypes.float8_e4m3fn).astype(np.float64) * np.repeat(np.exp2(scales.astype(np.float64) - 127.0), 8, axis=1)[..., None]
    return vals.transpose(0, 1, 3, 2).reshape(g * 512, n)


E2M1 = np.array([0.0, 0.5, 1.0, 1.5, 2.0, 3.0, 4.0, 6.0, -0.0, -0.5, -1.0, -1.5, -2.0, -3.0, -4.0, -6.0])


def pack_fp4(w):
    k, n = w.shape
    w = f64(np.asarray(w, np.float32).astype(ml_dtypes.bfloat16)).reshape(k // 32, 32, n)
    amax = np.abs(w).max(1)
    mant, ex = np.frexp(amax / 6.0)
    byte = np.clip(np.where(amax > 0, np.where(mant > 0.5, ex, ex - 1) + 127, 1), 1, 254)
    scaled = (w * np.exp2(127.0 - byte)[:, None, :]).reshape(k, n).astype(np.float32)
    c = np.ascontiguousarray(scaled.reshape(k // 512, 128, 4, n).transpose(0, 1, 3, 2)).astype(ml_dtypes.float4_e2m1fn).view(np.uint8) & 0xF
    words = (c[..., 0::2] | (c[..., 1::2] << 4)).reshape(k // 512, 128, 2 * n)
    return np.ascontiguousarray(words), np.ascontiguousarray(byte.astype(np.uint8).reshape(k // 512, 16, n))


def unpack_fp4(words, scales):
    g, _, n = scales.shape
    words = np.ascontiguousarray(words).reshape(g, 128, n, 2)
    nib = np.empty((g, 128, n, 4), np.uint8)
    nib[..., 0::2] = words & 0xF
    nib[..., 1::2] = words >> 4
    vals = E2M1[nib] * np.repeat(np.exp2(scales.astype(np.float64) - 127.0), 8, axis=1)[..., None]
    return vals.transpose(0, 1, 3, 2).reshape(g * 512, n)


def relu(v):
    return np.maximum(v, 0.0)


def sigmoid(v):
    return 1.0 / (1.0 + np.exp(-np.maximum(v, -700.0)))

def planes(y):
    n, m = y.shape
    v = y.astype(np.float32).astype(ml_dtypes.bfloat16).astype(np.float64).reshape(n // 32, 32, m)
    top = np.abs(v).max(1)
    byte = np.clip(np.where(top > 0, np.frexp(top)[1] - 1 + 127 - 7, 1), 1, 254)
    codes = (v * np.exp2(127.0 - byte)[:, None, :]).reshape(n, m).astype(np.float32).astype(ml_dtypes.float8_e4m3fn).view(np.uint8)
    words = codes.reshape(n // 512, 128, 4, m).transpose(0, 1, 3, 2)
    return np.ascontiguousarray(words), np.ascontiguousarray(byte.astype(np.uint8).reshape(n // 512, 16, m))


K, T, S, N, H = 512, 2048, 512, 512, 512


def setup_inputs():
    n = np.random.standard_normal
    s = mx_kscale(K)[:, None]
    u = mx_kscale(H)
    packed_xT = pack_weight(n((K, T)) * s)
    packed_w1 = pack_fp4(n((K, H)) / np.sqrt(K) / s)
    packed_w2 = pack_fp4(n((K, H)) / np.sqrt(K) / s)
    packed_w3 = pack_fp4(n((H, N)) / np.sqrt(H) / u[:, None])
    return {
        "x_words": packed_xT[0],
        "x_scales": packed_xT[1],
        "w1_words": packed_w1[0],
        "w1_scales": packed_w1[1],
        "w2_words": packed_w2[0],
        "w2_scales": packed_w2[1],
        "gn": (np.random.uniform(0.5, 1.5, (H, 1)) * u[:, None]).astype(np.float32),
        "w3_words": packed_w3[0],
        "w3_scales": packed_w3[1],
        "offs": striped(np.random.permutation(T)[:S]),
        "two": striped(np.random.permutation(T)[:S]),
        "n1": striped8(np.stack([np.random.permutation(S) for _ in range(8)])),
        "n2": striped8(np.stack([np.random.permutation(S) for _ in range(8)])),
        "n3": striped8(np.stack([np.random.permutation(S) for _ in range(8)])),
        "n4": striped8(np.stack([np.random.permutation(S) for _ in range(8)])),
    }


def reference(x_words, x_scales, w1_words, w1_scales, w2_words, w2_scales, gn, w3_words, w3_scales, offs, two, n1, n2, n3, n4):
    xq = unpack_weight(x_words, x_scales)[:, unstriped(offs)]
    y = unpack_fp4(w1_words, w1_scales).T @ xq
    x_two = unpack_weight(x_words, x_scales)[:, unstriped(two)]
    d = unpack_fp4(w2_words, w2_scales).T @ x_two
    z = f64(gn) * (y + (sigmoid(d[np.arange(H)[:, None], runs(n2, H)] - d)) * (y[np.arange(H)[:, None], runs(n1, H)] - y))
    h = unpack_fp4(w3_words, w3_scales).T @ mxq(z, 0, "e4m3")
    pa = h - (h[np.arange(N)[:, None], runs(n3, N)])
    pb = h[np.arange(N)[:, None], runs(n4, N)] - h
    out_0 = relu(np.minimum(pa, pb)) - (relu(-1.0 * np.maximum(pa, pb)))
    return (out_0,) + planes(out_0)

@@ -1,0 +1,298 @@
+from contextlib import ExitStack
+
+import concourse.mybir as mybir
+
+K, T, S, N, H = 512, 2048, 512, 512, 512
+FLOPS = 2 * K * H * S * 2 + 2 * H * N * S
+
+F32 = mybir.dt.float32
+BF16 = mybir.dt.bfloat16
+I32 = mybir.dt.int32
+U32 = mybir.dt.uint32
+U16 = mybir.dt.uint16
+U8 = mybir.dt.uint8
+FP8X4 = mybir.dt.float8_e4m3fn_x4
+FP4X4 = mybir.dt.float4_e2m1fn_x4
+ALU = mybir.AluOpType
+ACT = mybir.ActivationFunctionType
+
+P = 128
+PACK = 4
+CHUNKS1 = [256,128,128]
+CHUNKS2 = [256,128,128]
+Y_ON_SCALAR = [4,5,6,7,8,9,10,11]
+YCOPY_ON_VECTOR = []
+HCOPY_ON_VECTOR = [10,11]
+H_ON_VECTOR = [1,3]
+DCOPY_ON_VECTOR = [1,2,3]
+D_ON_VECTOR = [2,3]
+H_BANKS = ["bank_b0", "bank_b1", "bank_b2", "bank_b3", "bank_a0", "bank_a1", "bank_a2", "bank_a3"]
+CAST_ON_SCALAR = [0,1]
+
+
+def bounds(widths):
+    return [(sum(widths[:i]), sum(widths[: i + 1])) for i in range(len(widths))]
+
+
+def tile_picked_twlpullbminmod_none_po_kernel(
+    tc, x_words, x_scales, w1_words, w1_scales, w2_words, w2_scales, gn, w3_words, w3_scales,
+    offs, two, n1, n2, n3, n4, out_0, out_1, out_2,
+):
+    nc = tc.nc
+    with ExitStack() as ctx:
+        held = ctx.enter_context(tc.tile_pool(name="held", bufs=1))
+        ring = ctx.enter_context(tc.tile_pool(name="ring", bufs=5))
+        psum = ctx.enter_context(tc.psum_pool(name="psum", bufs=1))
+
+        def load_list(name, src):
+            tile = held.tile([P, S // 16], U16, name=name)
+            nc.sync.dma_start(tile[:], src)
+            return tile
+
+        def load_scale_rows(queue, dst, src):
+            for q in range(4):
+                queue.dma_start(dst[32 * q : 32 * q + 4, :].bitcast(I32), src[0, 4 * q : 4 * q + 4, :].bitcast(I32))
+
+        def load_words(name, src):
+            tile = held.tile([P, 2 * H], U8, name=name)
+            nc.sync.dma_start(tile[:].bitcast(I32), src[0].bitcast(I32))
+            return tile
+
+        xw = held.tile([P, T], I32, name="xw")
+        xs = held.tile([P, T], U8, name="xs")
+        raw_scales = held.tile([P, 3 * H], U8, name="raw_scales")
+        nc.vector.memset(xs[:].bitcast(I32), 0)
+        nc.gpsimd.memset(raw_scales[:].bitcast(I32), 0)
+
+        nc.scalar.dma_start(xw[:], x_words[0].rearrange("p c r -> p (c r)").bitcast(I32))
+        two_list = load_list("two_list", two)
+        load_scale_rows(nc.sync, xs, x_scales)
+        w2_raw = load_words("w2_raw", w2_words)
+        load_scale_rows(nc.sync, raw_scales[:, 0:H], w2_scales)
+        offs_list = load_list("offs_list", offs)
+        w1_raw = load_words("w1_raw", w1_words)
+        load_scale_rows(nc.sync, raw_scales[:, H : 2 * H], w1_scales)
+        n2_list = load_list("n2_list", n2)
+        gain = held.tile([P, PACK], F32, name="gain")
+        nc.sync.dma_start(gain[:], gn.rearrange("(p t) o -> p (t o)", t=PACK))
+        n1_list = load_list("n1_list", n1)
+        w3_raw = load_words("w3_raw", w3_words)
+        load_scale_rows(nc.sync, raw_scales[:, 2 * H : 3 * H], w3_scales)
+        n3_list = load_list("n3_list", n3)
+        n4_list = load_list("n4_list", n4)
+
+        def deal(name, raw, i):
+            words = held.tile([P, 2 * H], U8, name=name + "_words", align_bytes=64)
+            scales = held.tile([P, H], U8, name=name + "_scales", align_bytes=64)
+            nc.scalar.copy(
+                words[:].bitcast(U16).rearrange("p (t m) -> p t m", t=PACK),
+                raw[:].bitcast(U16).rearrange("p (m t) -> p t m", t=PACK),
+            )
+            nc.gpsimd.tensor_copy(
+                scales[:].rearrange("p (t m) -> p t m", t=PACK),
+                raw_scales[:, i * H : (i + 1) * H].rearrange("p (m t) -> p t m", t=PACK),
+            )
+            return words, scales
+
+        def pick(name, lst):
+            words = held.tile([P, S], U32, name=name + "_words", align_bytes=64)
+            scales = held.tile([P, S], U8, name=name + "_scales", align_bytes=64)
+            nc.vector.tensor_copy(scales[:], xs[:].indirect(lst[:]))
+            nc.vector.tensor_copy(words[:], xw[:].bitcast(U32).indirect(lst[:]))
+            return words, scales
+
+        def product(out, w, t, words, scales):
+            nc.tensor.matmul_mx(
+                out=out,
+                lhsT=w[0][:, 2 * P * t : 2 * P * (t + 1)].bitcast(FP4X4),
+                lhsT_scale=w[1][:, P * t : P * (t + 1)],
+                rhs=words.bitcast(FP8X4),
+                rhs_scale=scales,
+                start=True,
+                stop=True,
+            )
+
+        w2 = deal("w2", w2_raw, 0)
+        x_two = pick("x_two", two_list)
+        d_ps = [psum.tile([P, S], F32, name="d_ps%d" % t, tag="bank_a%d" % t) for t in range(PACK)]
+        for t in range(PACK):
+            product(d_ps[t][:], w2, t, x_two[0][:], x_two[1][:])
+        w1 = deal("w1", w1_raw, 1)
+        x_offs = pick("x_offs", offs_list)
+        y_ps = [psum.tile([P, S], F32, name="y_ps%d" % t, tag="bank_b%d" % t) for t in range(PACK)]
+        for t in range(PACK):
+            product(y_ps[t][:], w1, t, x_offs[0][:], x_offs[1][:])
+
+        d_sb = [held.tile([P, S], F32, name="d_sb%d" % t) for t in range(PACK)]
+        y_sb = [held.tile([P, S], F32, name="y_sb%d" % t) for t in range(PACK)]
+        h_sb = [held.tile([P, S], F32, name="h_sb%d" % t) for t in range(PACK)]
+        far = held.tile([P, PACK, S], F32, name="far")
+        near = held.tile([P, PACK, S], F32, name="near")
+        z_bf = held.tile([P, S, PACK], BF16, name="z_bf", align_bytes=64)
+        z_words = held.tile([P, S], U32, name="z_words", align_bytes=64)
+        z_scales = held.tile([P, S], U8, name="z_scales", align_bytes=64)
+
+        spans = bounds(CHUNKS1)
+        d_far = held.tile([P, PACK, S], F32, name="d_far")
+        diff = held.tile([P, PACK, S], F32, name="diff")
+        gate = held.tile([P, PACK, S], F32, name="gate")
+        y_far = held.tile([P, PACK, S], F32, name="y_far")
+        h_ps = {}
+        state = {}
+
+        def look_up(on_vector, dst, window, lst, a, b):
+            picked = window[:].indirect(lst[:, a // 16 : b // 16])
+            if on_vector:
+                nc.vector.tensor_copy(dst, picked)
+            else:
+                nc.scalar.activation(dst, picked, ACT.Copy)
+
+        def leave(on_vector, dst, src):
+            if on_vector:
+                nc.vector.tensor_copy(dst, src)
+            else:
+                nc.scalar.copy(dst, src)
+
+        def d_side(t):
+            leave(t in DCOPY_ON_VECTOR, d_sb[t][:], d_ps[t][:])
+            for half in range(2):
+                a, b = half * S // 2, (half + 1) * S // 2
+                look_up(2 * t + half in D_ON_VECTOR, d_far[:, t, a:b], d_sb[t], n2_list, a, b)
+            nc.vector.tensor_tensor(diff[:, t, :], d_far[:, t, :], d_ps[t][:], ALU.subtract)
+
+        def y_side(t):
+            if t in YCOPY_ON_VECTOR:
+                nc.vector.tensor_scalar(y_sb[t][:], y_ps[t][:], gain[:, t : t + 1], None, ALU.mult)
+            else:
+                nc.scalar.activation(y_sb[t][:], y_ps[t][:], ACT.Copy, scale=gain[:, t : t + 1])
+            nc.scalar.activation(gate[:, t, :], diff[:, t, :], ACT.Sigmoid)
+
+        def own(t):
+            nc.vector.scalar_tensor_tensor(near[:, t, :], gate[:, t, :], 1.0, y_sb[t][:], ALU.subtract, ALU.mult)
+
+        def mix(c, t):
+            a, b = spans[c]
+            picked = y_sb[t][:].indirect(n1_list[:, a // 16 : b // 16])
+            if PACK * c + t in Y_ON_SCALAR:
+                nc.scalar.activation(y_far[:, t, a:b], picked, ACT.Copy)
+                picked = y_far[:, t, a:b]
+            nc.vector.tensor_tensor(far[:, t, a:b], picked, gate[:, t, a:b], ALU.mult)
+
+        def join(c):
+            a, b = spans[c]
+            nc.vector.tensor_tensor(
+                z_bf[:, a:b, :].rearrange("p (g i) t -> p g t i", i=4),
+                far[:, :, a:b].rearrange("p t (g i) -> p g t i", i=4),
+                near[:, :, a:b].rearrange("p t (g i) -> p g t i", i=4),
+                ALU.subtract,
+            )
+
+        def layer(c):
+            a, b = spans[c]
+            nc.vector.quantize_mx(
+                out=z_words[:, a:b].bitcast(FP8X4),
+                scales=z_scales[:, a:b],
+                in_=z_bf[:, a:b, :].rearrange("p c t -> p (c t)"),
+            )
+            for u in range(2):
+                h_ps[c, u] = psum.tile([P, 2, b - a], F32, name="h_ps%d%d" % (c, u), tag=H_BANKS[2 * c + u])
+            for t in range(PACK):
+                product(h_ps[c, t // 2][:, t % 2, :], state["w3"], t, z_words[:, a:b], z_scales[:, a:b])
+            for t in range(PACK):
+                leave(c * PACK + t in HCOPY_ON_VECTOR, h_sb[t][:, a:b], h_ps[c, t // 2][:, t % 2, :])
+
+        for k in range(PACK + 2):
+            if k < PACK:
+                d_side(k)
+            if 0 <= k - 1 < PACK:
+                y_side(k - 1)
+            if 0 <= k - 2 < PACK:
+                own(k - 2)
+                mix(0, k - 2)
+        state["w3"] = deal("w3", w3_raw, 2)
+        for c in range(1, len(CHUNKS1) + 1):
+            more = c < len(CHUNKS1)
+            if more:
+                mix(c, 0)
+            join(c - 1)
+            if more:
+                mix(c, 1)
+            layer(c - 1)
+            if more:
+                mix(c, 2)
+                mix(c, 3)
+
+        res = held.tile([P, PACK, S], F32, name="res")
+        res_bf = held.tile([P, S, PACK], BF16, name="res_bf", align_bytes=64)
+        res_words = held.tile([P, S], U32, name="res_words", align_bytes=64)
+        res_scales = held.tile([P, S], U8, name="res_scales", align_bytes=64)
+        out_rows = out_0.rearrange("(p t) c -> p t c", t=PACK)
+        out_words = out_1[0].rearrange("p c r -> p (c r)").bitcast(I32)
+
+        steps2 = [(c, u) for c in range(len(CHUNKS2)) for u in range(2)]
+        spans2 = bounds(CHUNKS2)
+        pa = held.tile([P, PACK, S], F32, name="pa")
+        pb = held.tile([P, PACK, S], F32, name="pb")
+        capped = held.tile([P, PACK, S], F32, name="capped")
+
+        def slopes(k):
+            c, u = steps2[k]
+            a, b = spans2[c]
+            source = [i for i, (lo, hi) in enumerate(spans) if lo <= a < hi][0]
+            h_here = h_ps[source, u][:, :, a - spans[source][0] : b - spans[source][0]]
+            for side, lst in enumerate((n3_list, n4_list)):
+                h_far = ring.tile([P, 2, b - a], F32, name="h_far")
+                for j in range(2):
+                    look_up(4 * k + 2 * side + j in H_ON_VECTOR, h_far[:, j, :], h_sb[2 * u + j], lst, a, b)
+                if side == 0:
+                    nc.vector.tensor_tensor(pa[:, 2 * u : 2 * u + 2, a:b], h_here, h_far[:], ALU.subtract)
+                else:
+                    nc.vector.tensor_tensor(pb[:, 2 * u : 2 * u + 2, a:b], h_far[:], h_here, ALU.subtract)
+
+        def upper(k):
+            c, u = steps2[k]
+            a, b = spans2[c]
+            rows = slice(2 * u, 2 * u + 2)
+            nc.vector.scalar_tensor_tensor(capped[:, rows, a:b], pb[:, rows, a:b], 0.0, pa[:, rows, a:b], ALU.max, ALU.min)
+
+        def lower(k):
+            c, u = steps2[k]
+            a, b = spans2[c]
+            rows = slice(2 * u, 2 * u + 2)
+            nc.vector.scalar_tensor_tensor(res[:, rows, a:b], pb[:, rows, a:b], 0.0, capped[:, rows, a:b], ALU.min, ALU.max)
+            nc.sync.dma_start(out_rows[:, rows, a:b], res[:, rows, a:b])
+
+        def cast(c):
+            a, b = spans2[c]
+            dst = res_bf[:, a:b, :].rearrange("p (g i) t -> p g t i", i=4)
+            src = res[:, :, a:b].rearrange("p t (g i) -> p g t i", i=4)
+            if c in CAST_ON_SCALAR:
+                nc.scalar.copy(dst, src)
+            else:
+                nc.vector.tensor_copy(dst, src)
+
+        def planes(c):
+            a, b = spans2[c]
+            nc.vector.quantize_mx(
+                out=res_words[:, a:b].bitcast(FP8X4),
+                scales=res_scales[:, a:b],
+                in_=res_bf[:, a:b, :].rearrange("p c t -> p (c t)"),
+            )
+            nc.sync.dma_start(out_words[:, a:b], res_words[:, a:b].bitcast(I32))
+
+        n_steps = len(steps2)
+        for k in range(n_steps + 3):
+            if k < n_steps:
+                slopes(k)
+            if 0 <= k - 1 < n_steps:
+                lower(k - 1)
+            if k < n_steps:
+                upper(k)
+            if k - 2 >= 0 and (k - 2) % 2 == 1 and k - 2 < n_steps:
+                cast((k - 2) // 2)
+            if k - 3 >= 0 and (k - 3) % 2 == 1:
+                planes((k - 3) // 2)
+
+        for q in range(4):
+            queue = nc.scalar if q % 2 else nc.sync
+            queue.dma_start(out_2[0, 4 * q : 4 * q + 4, :].bitcast(I32), res_scales[32 * q : 32 * q + 4, :].bitcast(I32))

@@ -65,6 +65,10 @@ def tile_picked_twlpullbminmod_none_po_kernel(
         nc.gpsimd.memset(raw_scales[:].bitcast(I32), 0)
 
         nc.scalar.dma_start(xw[:], x_words[0].rearrange("p c r -> p (c r)").bitcast(I32))
+        warm_in = held.tile([P, 1], F32, name="warm_in")
+        warm_out = held.tile([P, 1], F32, name="warm_out")
+        nc.vector.memset(warm_in[:], 0.0)
+        nc.scalar.activation(warm_out[:], warm_in[:], ACT.Sigmoid)
         two_list = load_list("two_list", two)
         load_scale_rows(nc.sync, xs, x_scales)
         w2_raw = load_words("w2_raw", w2_words)

@@ -60,46 +60,49 @@ def tile_picked_twlpullbminmod_none_po_kernel(
 
         xw = held.tile([P, T], I32, name="xw")
         xs = held.tile([P, T], U8, name="xs")
-        raw_scales = held.tile([P, 3 * H], U8, name="raw_scales")
-        nc.vector.memset(xs[:].bitcast(I32), 0)
+        w2_raw_scales = held.tile([P, H], U8, name="w2_raw_scales", tag="reused", align_bytes=64)
+        raw_scales = held.tile([P, 2 * H], U8, name="raw_scales")
+        nc.vector.memset(xs[:, : T // 2].bitcast(I32), 0)
+        nc.gpsimd.memset(xs[:, T // 2 :].bitcast(I32), 0)
+        nc.vector.memset(w2_raw_scales[:].bitcast(I32), 0)
         nc.gpsimd.memset(raw_scales[:].bitcast(I32), 0)
 
-        nc.scalar.dma_start(xw[:], x_words[0].rearrange("p c r -> p (c r)").bitcast(I32))
         warm_in = held.tile([P, 1], F32, name="warm_in")
         warm_out = held.tile([P, 1], F32, name="warm_out")
         nc.vector.memset(warm_in[:], 0.0)
         nc.scalar.activation(warm_out[:], warm_in[:], ACT.Sigmoid)
         two_list = load_list("two_list", two)
-        load_scale_rows(nc.sync, xs, x_scales)
-        w2_raw = load_words("w2_raw", w2_words)
-        load_scale_rows(nc.sync, raw_scales[:, 0:H], w2_scales)
         offs_list = load_list("offs_list", offs)
-        w1_raw = load_words("w1_raw", w1_words)
-        load_scale_rows(nc.sync, raw_scales[:, H : 2 * H], w1_scales)
+        w2_raw = load_words("w2_raw", w2_words)
+        load_scale_rows(nc.sync, xs, x_scales)
+        nc.sync.dma_start(xw[:], x_words[0].rearrange("p c r -> p (c r)").bitcast(I32))
+        load_scale_rows(nc.sync, w2_raw_scales, w2_scales)
         n2_list = load_list("n2_list", n2)
+        w1_raw = load_words("w1_raw", w1_words)
         gain = held.tile([P, PACK], F32, name="gain")
         nc.sync.dma_start(gain[:], gn.rearrange("(p t) o -> p (t o)", t=PACK))
+        load_scale_rows(nc.sync, raw_scales[:, :H], w1_scales)
+        load_scale_rows(nc.sync, raw_scales[:, H:], w3_scales)
         n1_list = load_list("n1_list", n1)
         w3_raw = load_words("w3_raw", w3_words)
-        load_scale_rows(nc.sync, raw_scales[:, 2 * H : 3 * H], w3_scales)
         n3_list = load_list("n3_list", n3)
         n4_list = load_list("n4_list", n4)
 
-        def deal(name, raw, i):
+        def deal(name, raw, raw_bytes, engine):
             words = held.tile([P, 2 * H], U8, name=name + "_words", align_bytes=64)
             scales = held.tile([P, H], U8, name=name + "_scales", align_bytes=64)
             nc.scalar.copy(
                 words[:].bitcast(U16).rearrange("p (t m) -> p t m", t=PACK),
                 raw[:].bitcast(U16).rearrange("p (m t) -> p t m", t=PACK),
             )
-            nc.gpsimd.tensor_copy(
+            engine.tensor_copy(
                 scales[:].rearrange("p (t m) -> p t m", t=PACK),
-                raw_scales[:, i * H : (i + 1) * H].rearrange("p (m t) -> p t m", t=PACK),
+                raw_bytes.rearrange("p (m t) -> p t m", t=PACK),
             )
             return words, scales
 
-        def pick(name, lst):
-            words = held.tile([P, S], U32, name=name + "_words", align_bytes=64)
+        def pick(name, lst, tag):
+            words = held.tile([P, S], U32, name=name + "_words", tag=tag, align_bytes=64)
             scales = held.tile([P, S], U8, name=name + "_scales", align_bytes=64)
             nc.vector.tensor_copy(scales[:], xs[:].indirect(lst[:]))
             nc.vector.tensor_copy(words[:], xw[:].bitcast(U32).indirect(lst[:]))
@@ -116,13 +119,13 @@ def tile_picked_twlpullbminmod_none_po_kernel(
                 stop=True,
             )
 
-        w2 = deal("w2", w2_raw, 0)
-        x_two = pick("x_two", two_list)
+        w2 = deal("w2", w2_raw, w2_raw_scales[:], nc.vector)
+        x_two = pick("x_two", two_list, "x_two_words")
         d_ps = [psum.tile([P, S], F32, name="d_ps%d" % t, tag="bank_a%d" % t) for t in range(PACK)]
         for t in range(PACK):
             product(d_ps[t][:], w2, t, x_two[0][:], x_two[1][:])
-        w1 = deal("w1", w1_raw, 1)
-        x_offs = pick("x_offs", offs_list)
+        w1 = deal("w1", w1_raw, raw_scales[:, :H], nc.gpsimd)
+        x_offs = pick("x_offs", offs_list, "reused")
         y_ps = [psum.tile([P, S], F32, name="y_ps%d" % t, tag="bank_b%d" % t) for t in range(PACK)]
         for t in range(PACK):
             product(y_ps[t][:], w1, t, x_offs[0][:], x_offs[1][:])
@@ -213,7 +216,7 @@ def tile_picked_twlpullbminmod_none_po_kernel(
             if 0 <= k - 2 < PACK:
                 own(k - 2)
                 mix(0, k - 2)
-        state["w3"] = deal("w3", w3_raw, 2)
+        state["w3"] = deal("w3", w3_raw, raw_scales[:, H:], nc.gpsimd)
         for c in range(1, len(CHUNKS1) + 1):
             more = c < len(CHUNKS1)
             if more:

@@ -23,7 +23,7 @@ CHUNKS2 = [256,128,128]
 Y_ON_SCALAR = [4,5,6,7,8,9,10,11]
 YCOPY_ON_VECTOR = []
 HCOPY_ON_VECTOR = [10,11]
-H_ON_VECTOR = [1,3]
+H_ON_VECTOR = [1,3,5,7]
 DCOPY_ON_VECTOR = [1,2,3]
 D_ON_VECTOR = [2,3]
 H_BANKS = ["bank_b0", "bank_b1", "bank_b2", "bank_b3", "bank_a0", "bank_a1", "bank_a2", "bank_a3"]
@@ -49,9 +49,9 @@ def tile_picked_twlpullbminmod_none_po_kernel(
             nc.sync.dma_start(tile[:], src)
             return tile
 
-        def load_scale_rows(queue, dst, src):
+        def load_scale_rows(queues, dst, src):
             for q in range(4):
-                queue.dma_start(dst[32 * q : 32 * q + 4, :].bitcast(I32), src[0, 4 * q : 4 * q + 4, :].bitcast(I32))
+                queues[q].dma_start(dst[32 * q : 32 * q + 4, :].bitcast(I32), src[0, 4 * q : 4 * q + 4, :].bitcast(I32))
 
         def load_words(name, src):
             tile = held.tile([P, 2 * H], U8, name=name)
@@ -74,15 +74,15 @@ def tile_picked_twlpullbminmod_none_po_kernel(
         two_list = load_list("two_list", two)
         offs_list = load_list("offs_list", offs)
         w2_raw = load_words("w2_raw", w2_words)
-        load_scale_rows(nc.sync, xs, x_scales)
+        load_scale_rows([nc.sync] * 4, xs, x_scales)
         nc.sync.dma_start(xw[:], x_words[0].rearrange("p c r -> p (c r)").bitcast(I32))
-        load_scale_rows(nc.sync, w2_raw_scales, w2_scales)
-        n2_list = load_list("n2_list", n2)
+        load_scale_rows([nc.sync] * 4, w2_raw_scales, w2_scales)
         w1_raw = load_words("w1_raw", w1_words)
+        load_scale_rows([nc.sync, nc.sync, nc.gpsimd, nc.gpsimd], raw_scales[:, :H], w1_scales)
+        n2_list = load_list("n2_list", n2)
         gain = held.tile([P, PACK], F32, name="gain")
         nc.sync.dma_start(gain[:], gn.rearrange("(p t) o -> p (t o)", t=PACK))
-        load_scale_rows(nc.sync, raw_scales[:, :H], w1_scales)
-        load_scale_rows(nc.sync, raw_scales[:, H:], w3_scales)
+        load_scale_rows([nc.sync] * 4, raw_scales[:, H:], w3_scales)
         n1_list = load_list("n1_list", n1)
         w3_raw = load_words("w3_raw", w3_words)
         n3_list = load_list("n3_list", n3)
@@ -124,8 +124,8 @@ def tile_picked_twlpullbminmod_none_po_kernel(
         d_ps = [psum.tile([P, S], F32, name="d_ps%d" % t, tag="bank_a%d" % t) for t in range(PACK)]
         for t in range(PACK):
             product(d_ps[t][:], w2, t, x_two[0][:], x_two[1][:])
-        w1 = deal("w1", w1_raw, raw_scales[:, :H], nc.gpsimd)
         x_offs = pick("x_offs", offs_list, "reused")
+        w1 = deal("w1", w1_raw, raw_scales[:, :H], nc.vector)
         y_ps = [psum.tile([P, S], F32, name="y_ps%d" % t, tag="bank_b%d" % t) for t in range(PACK)]
         for t in range(PACK):
             product(y_ps[t][:], w1, t, x_offs[0][:], x_offs[1][:])
@@ -237,7 +237,7 @@ def tile_picked_twlpullbminmod_none_po_kernel(
         out_words = out_1[0].rearrange("p c r -> p (c r)").bitcast(I32)
 
         steps2 = [(c, u) for c in range(len(CHUNKS2)) for u in range(2)]
-        spans2 = bounds(CHUNKS2)
+        spans2 = [spans[1], spans[0], spans[2]]
         pa = held.tile([P, PACK, S], F32, name="pa")
         pb = held.tile([P, PACK, S], F32, name="pb")
         capped = held.tile([P, PACK, S], F32, name="capped")

@@ -18,20 +18,14 @@ ACT = mybir.ActivationFunctionType
 
 P = 128
 PACK = 4
-CHUNKS1 = [256,128,128]
-CHUNKS2 = [256,128,128]
-Y_ON_SCALAR = [4,5,6,7,8,9,10,11]
-YCOPY_ON_VECTOR = []
-HCOPY_ON_VECTOR = [10,11]
-H_ON_VECTOR = [1,3,5,7]
-DCOPY_ON_VECTOR = [1,2,3]
-D_ON_VECTOR = [2,3]
-H_BANKS = ["bank_b0", "bank_b1", "bank_b2", "bank_b3", "bank_a0", "bank_a1", "bank_a2", "bank_a3"]
-CAST_ON_SCALAR = [0,1]
-
-
-def bounds(widths):
-    return [(sum(widths[:i]), sum(widths[: i + 1])) for i in range(len(widths))]
+QUADRANTS = 4
+LIST_ROWS = 16
+LINE = 4
+Z_CHUNKS = [(0, 256), (256, 384), (384, 512)]
+OUT_CHUNKS = [1, 0, 2]
+D_TILE_ON_VECTOR = 1
+H_FAR_BUFS = 5
+H_BANKS = ["bank_b0", "bank_b1", "bank_b2", "bank_b3", "bank_a0", "bank_a1"]
 
 
 def tile_picked_twlpullbminmod_none_po_kernel(
@@ -41,16 +35,16 @@ def tile_picked_twlpullbminmod_none_po_kernel(
     nc = tc.nc
     with ExitStack() as ctx:
         held = ctx.enter_context(tc.tile_pool(name="held", bufs=1))
-        ring = ctx.enter_context(tc.tile_pool(name="ring", bufs=5))
+        ring = ctx.enter_context(tc.tile_pool(name="ring", bufs=H_FAR_BUFS))
         psum = ctx.enter_context(tc.psum_pool(name="psum", bufs=1))
 
         def load_list(name, src):
-            tile = held.tile([P, S // 16], U16, name=name)
+            tile = held.tile([P, S // LIST_ROWS], U16, name=name)
             nc.sync.dma_start(tile[:], src)
             return tile
 
         def load_scale_rows(queues, dst, src):
-            for q in range(4):
+            for q in range(QUADRANTS):
                 queues[q].dma_start(dst[32 * q : 32 * q + 4, :].bitcast(I32), src[0, 4 * q : 4 * q + 4, :].bitcast(I32))
 
         def load_words(name, src):
@@ -71,48 +65,49 @@ def tile_picked_twlpullbminmod_none_po_kernel(
         warm_out = held.tile([P, 1], F32, name="warm_out")
         nc.vector.memset(warm_in[:], 0.0)
         nc.scalar.activation(warm_out[:], warm_in[:], ACT.Sigmoid)
+
         two_list = load_list("two_list", two)
         offs_list = load_list("offs_list", offs)
         w2_raw = load_words("w2_raw", w2_words)
-        load_scale_rows([nc.sync] * 4, xs, x_scales)
+        load_scale_rows([nc.sync] * QUADRANTS, xs, x_scales)
         nc.sync.dma_start(xw[:], x_words[0].rearrange("p c r -> p (c r)").bitcast(I32))
-        load_scale_rows([nc.sync] * 4, w2_raw_scales, w2_scales)
+        load_scale_rows([nc.sync] * QUADRANTS, w2_raw_scales, w2_scales)
         w1_raw = load_words("w1_raw", w1_words)
         load_scale_rows([nc.sync, nc.sync, nc.gpsimd, nc.gpsimd], raw_scales[:, :H], w1_scales)
         n2_list = load_list("n2_list", n2)
         gain = held.tile([P, PACK], F32, name="gain")
         nc.sync.dma_start(gain[:], gn.rearrange("(p t) o -> p (t o)", t=PACK))
-        load_scale_rows([nc.sync] * 4, raw_scales[:, H:], w3_scales)
+        load_scale_rows([nc.sync] * QUADRANTS, raw_scales[:, H:], w3_scales)
         n1_list = load_list("n1_list", n1)
         w3_raw = load_words("w3_raw", w3_words)
         n3_list = load_list("n3_list", n3)
         n4_list = load_list("n4_list", n4)
 
-        def deal(name, raw, raw_bytes, engine):
+        def deal(name, raw_words, raw_bytes, byte_engine):
             words = held.tile([P, 2 * H], U8, name=name + "_words", align_bytes=64)
             scales = held.tile([P, H], U8, name=name + "_scales", align_bytes=64)
             nc.scalar.copy(
                 words[:].bitcast(U16).rearrange("p (t m) -> p t m", t=PACK),
-                raw[:].bitcast(U16).rearrange("p (m t) -> p t m", t=PACK),
+                raw_words[:].bitcast(U16).rearrange("p (m t) -> p t m", t=PACK),
             )
-            engine.tensor_copy(
+            byte_engine.tensor_copy(
                 scales[:].rearrange("p (t m) -> p t m", t=PACK),
                 raw_bytes.rearrange("p (m t) -> p t m", t=PACK),
             )
             return words, scales
 
-        def pick(name, lst, tag):
-            words = held.tile([P, S], U32, name=name + "_words", tag=tag, align_bytes=64)
+        def pick(name, lst, words_tag):
+            words = held.tile([P, S], U32, name=name + "_words", tag=words_tag, align_bytes=64)
             scales = held.tile([P, S], U8, name=name + "_scales", align_bytes=64)
             nc.vector.tensor_copy(scales[:], xs[:].indirect(lst[:]))
             nc.vector.tensor_copy(words[:], xw[:].bitcast(U32).indirect(lst[:]))
             return words, scales
 
-        def product(out, w, t, words, scales):
+        def product(out, weight, t, words, scales):
             nc.tensor.matmul_mx(
                 out=out,
-                lhsT=w[0][:, 2 * P * t : 2 * P * (t + 1)].bitcast(FP4X4),
-                lhsT_scale=w[1][:, P * t : P * (t + 1)],
+                lhsT=weight[0][:, 2 * P * t : 2 * P * (t + 1)].bitcast(FP4X4),
+                lhsT_scale=weight[1][:, P * t : P * (t + 1)],
                 rhs=words.bitcast(FP8X4),
                 rhs_scale=scales,
                 start=True,
@@ -138,64 +133,62 @@ def tile_picked_twlpullbminmod_none_po_kernel(
         z_bf = held.tile([P, S, PACK], BF16, name="z_bf", align_bytes=64)
         z_words = held.tile([P, S], U32, name="z_words", align_bytes=64)
         z_scales = held.tile([P, S], U8, name="z_scales", align_bytes=64)
-
-        spans = bounds(CHUNKS1)
         d_far = held.tile([P, PACK, S], F32, name="d_far")
         diff = held.tile([P, PACK, S], F32, name="diff")
         gate = held.tile([P, PACK, S], F32, name="gate")
         y_far = held.tile([P, PACK, S], F32, name="y_far")
         h_ps = {}
-        state = {}
+        twin_chunk = OUT_CHUNKS[0]
+        h_twin = held.tile([P, PACK, Z_CHUNKS[twin_chunk][1] - Z_CHUNKS[twin_chunk][0]], F32, name="h_twin")
 
-        def look_up(on_vector, dst, window, lst, a, b):
-            picked = window[:].indirect(lst[:, a // 16 : b // 16])
+        def picked(window, lst, a, b):
+            return window[:].indirect(lst[:, a // LIST_ROWS : b // LIST_ROWS])
+
+        def look_up(on_vector, dst, src):
             if on_vector:
-                nc.vector.tensor_copy(dst, picked)
+                nc.vector.tensor_copy(dst, src)
             else:
-                nc.scalar.activation(dst, picked, ACT.Copy)
+                nc.scalar.activation(dst, src, ACT.Copy)
 
-        def leave(on_vector, dst, src):
+        def leave_psum(on_vector, dst, src):
             if on_vector:
                 nc.vector.tensor_copy(dst, src)
             else:
                 nc.scalar.copy(dst, src)
 
+        def side_by_side(tile, a, b):
+            return tile[:, a:b, :].rearrange("p (g i) t -> p g t i", i=LINE)
+
+        def tile_by_tile(tile, a, b):
+            return tile[:, :, a:b].rearrange("p t (g i) -> p g t i", i=LINE)
+
         def d_side(t):
-            leave(t in DCOPY_ON_VECTOR, d_sb[t][:], d_ps[t][:])
-            for half in range(2):
-                a, b = half * S // 2, (half + 1) * S // 2
-                look_up(2 * t + half in D_ON_VECTOR, d_far[:, t, a:b], d_sb[t], n2_list, a, b)
+            leave_psum(t > 0, d_sb[t][:], d_ps[t][:])
+            for a, b in ((0, S // 2), (S // 2, S)):
+                look_up(t == D_TILE_ON_VECTOR, d_far[:, t, a:b], picked(d_sb[t], n2_list, a, b))
             nc.vector.tensor_tensor(diff[:, t, :], d_far[:, t, :], d_ps[t][:], ALU.subtract)
 
         def y_side(t):
-            if t in YCOPY_ON_VECTOR:
-                nc.vector.tensor_scalar(y_sb[t][:], y_ps[t][:], gain[:, t : t + 1], None, ALU.mult)
-            else:
-                nc.scalar.activation(y_sb[t][:], y_ps[t][:], ACT.Copy, scale=gain[:, t : t + 1])
+            nc.scalar.activation(y_sb[t][:], y_ps[t][:], ACT.Copy, scale=gain[:, t : t + 1])
             nc.scalar.activation(gate[:, t, :], diff[:, t, :], ACT.Sigmoid)
 
-        def own(t):
+        def near_term(t):
             nc.vector.scalar_tensor_tensor(near[:, t, :], gate[:, t, :], 1.0, y_sb[t][:], ALU.subtract, ALU.mult)
 
-        def mix(c, t):
-            a, b = spans[c]
-            picked = y_sb[t][:].indirect(n1_list[:, a // 16 : b // 16])
-            if PACK * c + t in Y_ON_SCALAR:
-                nc.scalar.activation(y_far[:, t, a:b], picked, ACT.Copy)
-                picked = y_far[:, t, a:b]
-            nc.vector.tensor_tensor(far[:, t, a:b], picked, gate[:, t, a:b], ALU.mult)
+        def far_term(c, t):
+            a, b = Z_CHUNKS[c]
+            y_there = picked(y_sb[t], n1_list, a, b)
+            if c > 0:
+                nc.scalar.activation(y_far[:, t, a:b], y_there, ACT.Copy)
+                y_there = y_far[:, t, a:b]
+            nc.vector.tensor_tensor(far[:, t, a:b], y_there, gate[:, t, a:b], ALU.mult)
 
         def join(c):
-            a, b = spans[c]
-            nc.vector.tensor_tensor(
-                z_bf[:, a:b, :].rearrange("p (g i) t -> p g t i", i=4),
-                far[:, :, a:b].rearrange("p t (g i) -> p g t i", i=4),
-                near[:, :, a:b].rearrange("p t (g i) -> p g t i", i=4),
-                ALU.subtract,
-            )
+            a, b = Z_CHUNKS[c]
+            nc.vector.tensor_tensor(side_by_side(z_bf, a, b), tile_by_tile(far, a, b), tile_by_tile(near, a, b), ALU.subtract)
 
-        def layer(c):
-            a, b = spans[c]
+        def layer(c, w3):
+            a, b = Z_CHUNKS[c]
             nc.vector.quantize_mx(
                 out=z_words[:, a:b].bitcast(FP8X4),
                 scales=z_scales[:, a:b],
@@ -204,9 +197,12 @@ def tile_picked_twlpullbminmod_none_po_kernel(
             for u in range(2):
                 h_ps[c, u] = psum.tile([P, 2, b - a], F32, name="h_ps%d%d" % (c, u), tag=H_BANKS[2 * c + u])
             for t in range(PACK):
-                product(h_ps[c, t // 2][:, t % 2, :], state["w3"], t, z_words[:, a:b], z_scales[:, a:b])
+                product(h_ps[c, t // 2][:, t % 2, :], w3, t, z_words[:, a:b], z_scales[:, a:b])
             for t in range(PACK):
-                leave(c * PACK + t in HCOPY_ON_VECTOR, h_sb[t][:, a:b], h_ps[c, t // 2][:, t % 2, :])
+                leave_psum(c == len(Z_CHUNKS) - 1 and t >= 2, h_sb[t][:, a:b], h_ps[c, t // 2][:, t % 2, :])
+            if c == twin_chunk:
+                for u in range(2):
+                    nc.scalar.copy(h_twin[:, 2 * u : 2 * u + 2, :], h_ps[c, u][:])
 
         for k in range(PACK + 2):
             if k < PACK:
@@ -214,20 +210,18 @@ def tile_picked_twlpullbminmod_none_po_kernel(
             if 0 <= k - 1 < PACK:
                 y_side(k - 1)
             if 0 <= k - 2 < PACK:
-                own(k - 2)
-                mix(0, k - 2)
-        state["w3"] = deal("w3", w3_raw, raw_scales[:, H:], nc.gpsimd)
-        for c in range(1, len(CHUNKS1) + 1):
-            more = c < len(CHUNKS1)
-            if more:
-                mix(c, 0)
+                near_term(k - 2)
+                far_term(0, k - 2)
+        w3 = deal("w3", w3_raw, raw_scales[:, H:], nc.gpsimd)
+        for c in range(1, len(Z_CHUNKS)):
+            far_term(c, 0)
             join(c - 1)
-            if more:
-                mix(c, 1)
-            layer(c - 1)
-            if more:
-                mix(c, 2)
-                mix(c, 3)
+            far_term(c, 1)
+            layer(c - 1, w3)
+            far_term(c, 2)
+            far_term(c, 3)
+        join(len(Z_CHUNKS) - 1)
+        layer(len(Z_CHUNKS) - 1, w3)
 
         res = held.tile([P, PACK, S], F32, name="res")
         res_bf = held.tile([P, S, PACK], BF16, name="res_bf", align_bytes=64)
@@ -235,51 +229,52 @@ def tile_picked_twlpullbminmod_none_po_kernel(
         res_scales = held.tile([P, S], U8, name="res_scales", align_bytes=64)
         out_rows = out_0.rearrange("(p t) c -> p t c", t=PACK)
         out_words = out_1[0].rearrange("p c r -> p (c r)").bitcast(I32)
-
-        steps2 = [(c, u) for c in range(len(CHUNKS2)) for u in range(2)]
-        spans2 = [spans[1], spans[0], spans[2]]
         pa = held.tile([P, PACK, S], F32, name="pa")
         pb = held.tile([P, PACK, S], F32, name="pb")
         capped = held.tile([P, PACK, S], F32, name="capped")
 
+        steps = [(c, u) for c in OUT_CHUNKS for u in range(2)]
+
+        def h_far(lst, c, u, second_on_vector):
+            a, b = Z_CHUNKS[c]
+            there = ring.tile([P, 2, b - a], F32, name="h_far")
+            for j in range(2):
+                look_up(second_on_vector and j == 1, there[:, j, :], picked(h_sb[2 * u + j], lst, a, b))
+            return there[:]
+
         def slopes(k):
-            c, u = steps2[k]
-            a, b = spans2[c]
-            source = [i for i, (lo, hi) in enumerate(spans) if lo <= a < hi][0]
-            h_here = h_ps[source, u][:, :, a - spans[source][0] : b - spans[source][0]]
-            for side, lst in enumerate((n3_list, n4_list)):
-                h_far = ring.tile([P, 2, b - a], F32, name="h_far")
-                for j in range(2):
-                    look_up(4 * k + 2 * side + j in H_ON_VECTOR, h_far[:, j, :], h_sb[2 * u + j], lst, a, b)
-                if side == 0:
-                    nc.vector.tensor_tensor(pa[:, 2 * u : 2 * u + 2, a:b], h_here, h_far[:], ALU.subtract)
-                else:
-                    nc.vector.tensor_tensor(pb[:, 2 * u : 2 * u + 2, a:b], h_far[:], h_here, ALU.subtract)
+            c, u = steps[k]
+            a, b = Z_CHUNKS[c]
+            rows = slice(2 * u, 2 * u + 2)
+            nc.vector.tensor_tensor(pa[:, rows, a:b], h_ps[c, u][:], h_far(n3_list, c, u, k == 0), ALU.subtract)
+            if c == twin_chunk:
+                for t in (2 * u, 2 * u + 1):
+                    nc.vector.tensor_tensor(pb[:, t, a:b], picked(h_sb[t], n4_list, a, b), h_twin[:, t, :], ALU.subtract)
+            else:
+                nc.vector.tensor_tensor(pb[:, rows, a:b], h_far(n4_list, c, u, False), h_ps[c, u][:], ALU.subtract)
 
         def upper(k):
-            c, u = steps2[k]
-            a, b = spans2[c]
+            c, u = steps[k]
+            a, b = Z_CHUNKS[c]
             rows = slice(2 * u, 2 * u + 2)
             nc.vector.scalar_tensor_tensor(capped[:, rows, a:b], pb[:, rows, a:b], 0.0, pa[:, rows, a:b], ALU.max, ALU.min)
 
         def lower(k):
-            c, u = steps2[k]
-            a, b = spans2[c]
+            c, u = steps[k]
+            a, b = Z_CHUNKS[c]
             rows = slice(2 * u, 2 * u + 2)
             nc.vector.scalar_tensor_tensor(res[:, rows, a:b], pb[:, rows, a:b], 0.0, capped[:, rows, a:b], ALU.min, ALU.max)
             nc.sync.dma_start(out_rows[:, rows, a:b], res[:, rows, a:b])
 
-        def cast(c):
-            a, b = spans2[c]
-            dst = res_bf[:, a:b, :].rearrange("p (g i) t -> p g t i", i=4)
-            src = res[:, :, a:b].rearrange("p t (g i) -> p g t i", i=4)
-            if c in CAST_ON_SCALAR:
-                nc.scalar.copy(dst, src)
+        def round_out(c):
+            a, b = Z_CHUNKS[c]
+            if c == OUT_CHUNKS[-1]:
+                nc.vector.tensor_copy(side_by_side(res_bf, a, b), tile_by_tile(res, a, b))
             else:
-                nc.vector.tensor_copy(dst, src)
+                nc.scalar.copy(side_by_side(res_bf, a, b), tile_by_tile(res, a, b))
 
-        def planes(c):
-            a, b = spans2[c]
+        def quantise_out(c):
+            a, b = Z_CHUNKS[c]
             nc.vector.quantize_mx(
                 out=res_words[:, a:b].bitcast(FP8X4),
                 scales=res_scales[:, a:b],
@@ -287,19 +282,18 @@ def tile_picked_twlpullbminmod_none_po_kernel(
             )
             nc.sync.dma_start(out_words[:, a:b], res_words[:, a:b].bitcast(I32))
 
-        n_steps = len(steps2)
-        for k in range(n_steps + 3):
-            if k < n_steps:
+        for k in range(len(steps) + 3):
+            if k < len(steps):
                 slopes(k)
-            if 0 <= k - 1 < n_steps:
+            if 0 <= k - 1 < len(steps):
                 lower(k - 1)
-            if k < n_steps:
+            if k < len(steps):
                 upper(k)
-            if k - 2 >= 0 and (k - 2) % 2 == 1 and k - 2 < n_steps:
-                cast((k - 2) // 2)
-            if k - 3 >= 0 and (k - 3) % 2 == 1:
-                planes((k - 3) // 2)
+            if 0 <= k - 2 < len(steps) and steps[k - 2][1] == 1:
+                round_out(steps[k - 2][0])
+            if 0 <= k - 3 < len(steps) and steps[k - 3][1] == 1:
+                quantise_out(steps[k - 3][0])
 
-        for q in range(4):
+        for q in range(QUADRANTS):
             queue = nc.scalar if q % 2 else nc.sync
             queue.dma_start(out_2[0, 4 * q : 4 * q + 4, :].bitcast(I32), res_scales[32 * q : 32 * q + 4, :].bitcast(I32))

from contextlib import ExitStack

import concourse.mybir as mybir

K, T, S, N, H = 512, 2048, 512, 512, 512
FLOPS = 2 * K * H * S * 2 + 2 * H * N * S

F32 = mybir.dt.float32
BF16 = mybir.dt.bfloat16
I32 = mybir.dt.int32
U32 = mybir.dt.uint32
U16 = mybir.dt.uint16
U8 = mybir.dt.uint8
FP8X4 = mybir.dt.float8_e4m3fn_x4
FP4X4 = mybir.dt.float4_e2m1fn_x4
ALU = mybir.AluOpType
ACT = mybir.ActivationFunctionType

P = 128
PACK = 4
QUADRANTS = 4
LIST_ROWS = 16
LINE = 4
Z_CHUNKS = [(0, 256), (256, 384), (384, 512)]
OUT_CHUNKS = [1, 0, 2]
D_TILE_ON_VECTOR = 1
H_FAR_BUFS = 5
H_BANKS = ["bank_b0", "bank_b1", "bank_b2", "bank_b3", "bank_a0", "bank_a1"]


def tile_picked_twlpullbminmod_none_po_kernel(
    tc, x_words, x_scales, w1_words, w1_scales, w2_words, w2_scales, gn, w3_words, w3_scales,
    offs, two, n1, n2, n3, n4, out_0, out_1, out_2,
):
    nc = tc.nc
    with ExitStack() as ctx:
        held = ctx.enter_context(tc.tile_pool(name="held", bufs=1))
        ring = ctx.enter_context(tc.tile_pool(name="ring", bufs=H_FAR_BUFS))
        psum = ctx.enter_context(tc.psum_pool(name="psum", bufs=1))

        def load_list(name, src):
            tile = held.tile([P, S // LIST_ROWS], U16, name=name)
            nc.sync.dma_start(tile[:], src)
            return tile

        def load_scale_rows(queues, dst, src):
            for q in range(QUADRANTS):
                queues[q].dma_start(dst[32 * q : 32 * q + 4, :].bitcast(I32), src[0, 4 * q : 4 * q + 4, :].bitcast(I32))

        def load_words(name, src):
            tile = held.tile([P, 2 * H], U8, name=name)
            nc.sync.dma_start(tile[:].bitcast(I32), src[0].bitcast(I32))
            return tile

        xw = held.tile([P, T], I32, name="xw")
        xs = held.tile([P, T], U8, name="xs")
        w2_raw_scales = held.tile([P, H], U8, name="w2_raw_scales", tag="reused", align_bytes=64)
        raw_scales = held.tile([P, 2 * H], U8, name="raw_scales")
        nc.vector.memset(xs[:, : T // 2].bitcast(I32), 0)
        nc.gpsimd.memset(xs[:, T // 2 :].bitcast(I32), 0)
        nc.vector.memset(w2_raw_scales[:].bitcast(I32), 0)
        nc.gpsimd.memset(raw_scales[:].bitcast(I32), 0)

        warm_in = held.tile([P, 1], F32, name="warm_in")
        warm_out = held.tile([P, 1], F32, name="warm_out")
        nc.vector.memset(warm_in[:], 0.0)
        nc.scalar.activation(warm_out[:], warm_in[:], ACT.Sigmoid)

        two_list = load_list("two_list", two)
        offs_list = load_list("offs_list", offs)
        w2_raw = load_words("w2_raw", w2_words)
        load_scale_rows([nc.sync] * QUADRANTS, xs, x_scales)
        nc.sync.dma_start(xw[:], x_words[0].rearrange("p c r -> p (c r)").bitcast(I32))
        load_scale_rows([nc.sync] * QUADRANTS, w2_raw_scales, w2_scales)
        w1_raw = load_words("w1_raw", w1_words)
        load_scale_rows([nc.sync, nc.sync, nc.gpsimd, nc.gpsimd], raw_scales[:, :H], w1_scales)
        n2_list = load_list("n2_list", n2)
        gain = held.tile([P, PACK], F32, name="gain")
        nc.sync.dma_start(gain[:], gn.rearrange("(p t) o -> p (t o)", t=PACK))
        load_scale_rows([nc.sync] * QUADRANTS, raw_scales[:, H:], w3_scales)
        n1_list = load_list("n1_list", n1)
        w3_raw = load_words("w3_raw", w3_words)
        n3_list = load_list("n3_list", n3)
        n4_list = load_list("n4_list", n4)

        def deal(name, raw_words, raw_bytes, byte_engine):
            words = held.tile([P, 2 * H], U8, name=name + "_words", align_bytes=64)
            scales = held.tile([P, H], U8, name=name + "_scales", align_bytes=64)
            nc.scalar.copy(
                words[:].bitcast(U16).rearrange("p (t m) -> p t m", t=PACK),
                raw_words[:].bitcast(U16).rearrange("p (m t) -> p t m", t=PACK),
            )
            byte_engine.tensor_copy(
                scales[:].rearrange("p (t m) -> p t m", t=PACK),
                raw_bytes.rearrange("p (m t) -> p t m", t=PACK),
            )
            return words, scales

        def pick(name, lst, words_tag):
            words = held.tile([P, S], U32, name=name + "_words", tag=words_tag, align_bytes=64)
            scales = held.tile([P, S], U8, name=name + "_scales", align_bytes=64)
            nc.vector.tensor_copy(scales[:], xs[:].indirect(lst[:]))
            nc.vector.tensor_copy(words[:], xw[:].bitcast(U32).indirect(lst[:]))
            return words, scales

        def product(out, weight, t, words, scales):
            nc.tensor.matmul_mx(
                out=out,
                lhsT=weight[0][:, 2 * P * t : 2 * P * (t + 1)].bitcast(FP4X4),
                lhsT_scale=weight[1][:, P * t : P * (t + 1)],
                rhs=words.bitcast(FP8X4),
                rhs_scale=scales,
                start=True,
                stop=True,
            )

        w2 = deal("w2", w2_raw, w2_raw_scales[:], nc.vector)
        x_two = pick("x_two", two_list, "x_two_words")
        d_ps = [psum.tile([P, S], F32, name="d_ps%d" % t, tag="bank_a%d" % t) for t in range(PACK)]
        for t in range(PACK):
            product(d_ps[t][:], w2, t, x_two[0][:], x_two[1][:])
        x_offs = pick("x_offs", offs_list, "reused")
        w1 = deal("w1", w1_raw, raw_scales[:, :H], nc.vector)
        y_ps = [psum.tile([P, S], F32, name="y_ps%d" % t, tag="bank_b%d" % t) for t in range(PACK)]
        for t in range(PACK):
            product(y_ps[t][:], w1, t, x_offs[0][:], x_offs[1][:])

        d_sb = [held.tile([P, S], F32, name="d_sb%d" % t) for t in range(PACK)]
        y_sb = [held.tile([P, S], F32, name="y_sb%d" % t) for t in range(PACK)]
        h_sb = [held.tile([P, S], F32, name="h_sb%d" % t) for t in range(PACK)]
        far = held.tile([P, PACK, S], F32, name="far")
        near = held.tile([P, PACK, S], F32, name="near")
        z_bf = held.tile([P, S, PACK], BF16, name="z_bf", align_bytes=64)
        z_words = held.tile([P, S], U32, name="z_words", align_bytes=64)
        z_scales = held.tile([P, S], U8, name="z_scales", align_bytes=64)
        d_far = held.tile([P, PACK, S], F32, name="d_far")
        diff = held.tile([P, PACK, S], F32, name="diff")
        gate = held.tile([P, PACK, S], F32, name="gate")
        y_far = held.tile([P, PACK, S], F32, name="y_far")
        h_ps = {}
        twin_chunk = OUT_CHUNKS[0]
        h_twin = held.tile([P, PACK, Z_CHUNKS[twin_chunk][1] - Z_CHUNKS[twin_chunk][0]], F32, name="h_twin")

        def picked(window, lst, a, b):
            return window[:].indirect(lst[:, a // LIST_ROWS : b // LIST_ROWS])

        def look_up(on_vector, dst, src):
            if on_vector:
                nc.vector.tensor_copy(dst, src)
            else:
                nc.scalar.activation(dst, src, ACT.Copy)

        def leave_psum(on_vector, dst, src):
            if on_vector:
                nc.vector.tensor_copy(dst, src)
            else:
                nc.scalar.copy(dst, src)

        def side_by_side(tile, a, b):
            return tile[:, a:b, :].rearrange("p (g i) t -> p g t i", i=LINE)

        def tile_by_tile(tile, a, b):
            return tile[:, :, a:b].rearrange("p t (g i) -> p g t i", i=LINE)

        def d_side(t):
            leave_psum(t > 0, d_sb[t][:], d_ps[t][:])
            for a, b in ((0, S // 2), (S // 2, S)):
                look_up(t == D_TILE_ON_VECTOR, d_far[:, t, a:b], picked(d_sb[t], n2_list, a, b))
            nc.vector.tensor_tensor(diff[:, t, :], d_far[:, t, :], d_ps[t][:], ALU.subtract)

        def y_side(t):
            nc.scalar.activation(y_sb[t][:], y_ps[t][:], ACT.Copy, scale=gain[:, t : t + 1])
            nc.scalar.activation(gate[:, t, :], diff[:, t, :], ACT.Sigmoid)

        def near_term(t):
            nc.vector.scalar_tensor_tensor(near[:, t, :], gate[:, t, :], 1.0, y_sb[t][:], ALU.subtract, ALU.mult)

        def far_term(c, t):
            a, b = Z_CHUNKS[c]
            y_there = picked(y_sb[t], n1_list, a, b)
            if c > 0:
                nc.scalar.activation(y_far[:, t, a:b], y_there, ACT.Copy)
                y_there = y_far[:, t, a:b]
            nc.vector.tensor_tensor(far[:, t, a:b], y_there, gate[:, t, a:b], ALU.mult)

        def join(c):
            a, b = Z_CHUNKS[c]
            nc.vector.tensor_tensor(side_by_side(z_bf, a, b), tile_by_tile(far, a, b), tile_by_tile(near, a, b), ALU.subtract)

        def layer(c, w3):
            a, b = Z_CHUNKS[c]
            nc.vector.quantize_mx(
                out=z_words[:, a:b].bitcast(FP8X4),
                scales=z_scales[:, a:b],
                in_=z_bf[:, a:b, :].rearrange("p c t -> p (c t)"),
            )
            for u in range(2):
                h_ps[c, u] = psum.tile([P, 2, b - a], F32, name="h_ps%d%d" % (c, u), tag=H_BANKS[2 * c + u])
            for t in range(PACK):
                product(h_ps[c, t // 2][:, t % 2, :], w3, t, z_words[:, a:b], z_scales[:, a:b])
            for t in range(PACK):
                leave_psum(c == len(Z_CHUNKS) - 1 and t >= 2, h_sb[t][:, a:b], h_ps[c, t // 2][:, t % 2, :])
            if c == twin_chunk:
                for u in range(2):
                    nc.scalar.copy(h_twin[:, 2 * u : 2 * u + 2, :], h_ps[c, u][:])

        for k in range(PACK + 2):
            if k < PACK:
                d_side(k)
            if 0 <= k - 1 < PACK:
                y_side(k - 1)
            if 0 <= k - 2 < PACK:
                near_term(k - 2)
                far_term(0, k - 2)
        w3 = deal("w3", w3_raw, raw_scales[:, H:], nc.gpsimd)
        for c in range(1, len(Z_CHUNKS)):
            far_term(c, 0)
            join(c - 1)
            far_term(c, 1)
            layer(c - 1, w3)
            far_term(c, 2)
            far_term(c, 3)
        join(len(Z_CHUNKS) - 1)
        layer(len(Z_CHUNKS) - 1, w3)

        res = held.tile([P, PACK, S], F32, name="res")
        res_bf = held.tile([P, S, PACK], BF16, name="res_bf", align_bytes=64)
        res_words = held.tile([P, S], U32, name="res_words", align_bytes=64)
        res_scales = held.tile([P, S], U8, name="res_scales", align_bytes=64)
        out_rows = out_0.rearrange("(p t) c -> p t c", t=PACK)
        out_words = out_1[0].rearrange("p c r -> p (c r)").bitcast(I32)
        pa = held.tile([P, PACK, S], F32, name="pa")
        pb = held.tile([P, PACK, S], F32, name="pb")
        capped = held.tile([P, PACK, S], F32, name="capped")

        steps = [(c, u) for c in OUT_CHUNKS for u in range(2)]

        def h_far(lst, c, u, second_on_vector):
            a, b = Z_CHUNKS[c]
            there = ring.tile([P, 2, b - a], F32, name="h_far")
            for j in range(2):
                look_up(second_on_vector and j == 1, there[:, j, :], picked(h_sb[2 * u + j], lst, a, b))
            return there[:]

        def slopes(k):
            c, u = steps[k]
            a, b = Z_CHUNKS[c]
            rows = slice(2 * u, 2 * u + 2)
            nc.vector.tensor_tensor(pa[:, rows, a:b], h_ps[c, u][:], h_far(n3_list, c, u, k == 0), ALU.subtract)
            if c == twin_chunk:
                for t in (2 * u, 2 * u + 1):
                    nc.vector.tensor_tensor(pb[:, t, a:b], picked(h_sb[t], n4_list, a, b), h_twin[:, t, :], ALU.subtract)
            else:
                nc.vector.tensor_tensor(pb[:, rows, a:b], h_far(n4_list, c, u, False), h_ps[c, u][:], ALU.subtract)

        def upper(k):
            c, u = steps[k]
            a, b = Z_CHUNKS[c]
            rows = slice(2 * u, 2 * u + 2)
            nc.vector.scalar_tensor_tensor(capped[:, rows, a:b], pb[:, rows, a:b], 0.0, pa[:, rows, a:b], ALU.max, ALU.min)

        def lower(k):
            c, u = steps[k]
            a, b = Z_CHUNKS[c]
            rows = slice(2 * u, 2 * u + 2)
            nc.vector.scalar_tensor_tensor(res[:, rows, a:b], pb[:, rows, a:b], 0.0, capped[:, rows, a:b], ALU.min, ALU.max)
            nc.sync.dma_start(out_rows[:, rows, a:b], res[:, rows, a:b])

        def round_out(c):
            a, b = Z_CHUNKS[c]
            if c == OUT_CHUNKS[-1]:
                nc.vector.tensor_copy(side_by_side(res_bf, a, b), tile_by_tile(res, a, b))
            else:
                nc.scalar.copy(side_by_side(res_bf, a, b), tile_by_tile(res, a, b))

        def quantise_out(c):
            a, b = Z_CHUNKS[c]
            nc.vector.quantize_mx(
                out=res_words[:, a:b].bitcast(FP8X4),
                scales=res_scales[:, a:b],
                in_=res_bf[:, a:b, :].rearrange("p c t -> p (c t)"),
            )
            nc.sync.dma_start(out_words[:, a:b], res_words[:, a:b].bitcast(I32))

        for k in range(len(steps) + 3):
            if k < len(steps):
                slopes(k)
            if 0 <= k - 1 < len(steps):
                lower(k - 1)
            if k < len(steps):
                upper(k)
            if 0 <= k - 2 < len(steps) and steps[k - 2][1] == 1:
                round_out(steps[k - 2][0])
            if 0 <= k - 3 < len(steps) and steps[k - 3][1] == 1:
                quantise_out(steps[k - 3][0])

        for q in range(QUADRANTS):
            queue = nc.scalar if q % 2 else nc.sync
            queue.dma_start(out_2[0, 4 * q : 4 * q + 4, :].bitcast(I32), res_scales[32 * q : 32 * q + 4, :].bitcast(I32))
